import numpy as np
import ml_dtypes


def mxq(x, axis, fmt="e4m3"):
    dtype, down = {"e4m3": (ml_dtypes.float8_e4m3fn, 7), "e5m2": (ml_dtypes.float8_e5m2, 14)}[fmt]
    v = np.moveaxis(np.asarray(x, np.float32).astype(ml_dtypes.bfloat16).astype(np.float64), axis, -1)
    blocks = v.reshape(v.shape[:-1] + (-1, 32))
    amax = np.abs(blocks).max(-1, keepdims=True)
    byte = np.maximum(np.where(amax > 0, np.frexp(amax)[1] - 1 + 127, 0) - down, 1)
    scale = np.exp2(byte - 127.0)
    codes = (blocks / scale).astype(np.float32).astype(dtype).astype(np.float64)
    return np.moveaxis((codes * scale).reshape(v.shape), -1, axis)


WIDE = False


def mx_kscale(k):
    if not WIDE:
        return np.ones(k)
    levels = np.array([30, -30])
    if k % 512:
        return np.exp2(np.random.permutation(np.resize(levels, k // 32))).repeat(32)
    a = np.empty((k // 512, 16))
    for p in range(k // 512):
        a[p, :8] = np.random.permutation(np.resize(levels, 8))
        for g in range(8):
            far = levels[np.abs(levels - a[p, g]) >= 10]
            a[p, g + 8] = far[np.random.randint(len(far))]
    return np.exp2(a.ravel()).repeat(32)


def f64(x):
    return np.asarray(x).astype(np.float64)


def striped(idx):
    return np.tile(np.asarray(idx).reshape(-1, 16).T, (8, 1)).astype(np.uint16)


def unstriped(offs):
    return offs[:16].T.reshape(-1).astype(np.int64)


E2M1 = np.array([0.0, 0.5, 1.0, 1.5, 2.0, 3.0, 4.0, 6.0, -0.0, -0.5, -1.0, -1.5, -2.0, -3.0, -4.0, -6.0])


def pack_weight(w, fmt):
    k, n = w.shape
    w = f64(np.asarray(w, np.float32).astype(ml_dtypes.bfloat16)).reshape(k // 32, 32, n)
    amax = np.abs(w).max(1)
    if fmt in ("e4m3", "e5m2"):
        byte = np.frexp(amax)[1] - 1 + 127 - (7 if fmt == "e4m3" else 14)
    else:
        mant, ex = np.frexp(amax / 6.0)
        byte = np.where(mant > 0.5, ex, ex - 1) + 127
    byte = np.clip(np.where(amax > 0, byte, 1), 1, 254)
    scaled = (w * np.exp2(127.0 - byte)[:, None, :]).reshape(k, n).astype(np.float32)
    by_word = np.ascontiguousarray(scaled.reshape(k // 512, 128, 4, n).transpose(0, 1, 3, 2))
    if fmt in ("e4m3", "e5m2"):
        words = by_word.astype(ml_dtypes.float8_e4m3fn if fmt == "e4m3" else ml_dtypes.float8_e5m2).view(np.uint8)
    else:
        c = by_word.astype(ml_dtypes.float4_e2m1fn).view(np.uint8) & 0xF
        words = (c[..., 0::2] | (c[..., 1::2] << 4)).reshape(k // 512, 128, 2 * n)
    return np.ascontiguousarray(words), np.ascontiguousarray(byte.astype(np.uint8).reshape(k // 512, 16, n))


def unpack_weight(words, scales, fmt):
    g, _, n = scales.shape
    words = np.ascontiguousarray(words).reshape(g, 128, n, -1)
    if fmt in ("e4m3", "e5m2"):
        vals = words.view(ml_dtypes.float8_e4m3fn if fmt == "e4m3" else ml_dtypes.float8_e5m2).astype(np.float64)
    else:
        nib = np.empty((g, 128, n, 4), np.uint8)
        nib[..., 0::2] = words & 0xF
        nib[..., 1::2] = words >> 4
        vals = E2M1[nib]
    vals = vals * np.repeat(np.exp2(scales.astype(np.float64) - 127.0), 8, axis=1)[..., None]
    return vals.transpose(0, 1, 3, 2).reshape(g * 512, n)


K, T, J, I, R, E, S = 512, 512, 256, 256, 512, 32, 64


def setup_inputs():
    n = np.random.standard_normal
    idx = np.random.permutation(T)[:J]
    idx2 = np.random.permutation(T)[:I]
    fk = mx_kscale(K)
    fr = mx_kscale(R)
    xtp = pack_weight(n((K, T)) / fk[:, None], "e4m3")
    wap = pack_weight(n((K, R)) * 0.5 / np.sqrt(K) * fk[:, None] * fr, "e5m2")
    wbp = pack_weight(n((K, R)) * 1 / np.sqrt(K) * fk[:, None] / fr, "e2m1")
    return {
        "xt_words": xtp[0],
        "xt_scales": xtp[1],
        "wa_words": wap[0],
        "wa_scales": wap[1],
        "wb_words": wbp[0],
        "wb_scales": wbp[1],
        "cw1": (np.random.uniform(-1.0, 1.0, (1, I))).astype(np.float32),
        "offs": striped(idx),
        "offs2": striped(idx2),
    }


def reference(xt_words, xt_scales, wa_words, wa_scales, wb_words, wb_scales, cw1, offs, offs2):
    idx = unstriped(offs)
    idx2 = unstriped(offs2)
    xtu = unpack_weight(xt_words, xt_scales, "e4m3")
    wau = unpack_weight(wa_words, wa_scales, "e5m2")
    wbu = unpack_weight(wb_words, wb_scales, "e2m1")
    xtidxg = xtu[:, idx]
    za = wau.T @ xtidxg
    ma1 = za.reshape(R, E, J // E).mean(axis=2)
    ma2 = np.repeat(ma1, J // E, axis=1)
    ha = za - ma2
    xtidx2g = xtu[:, idx2]
    zb = wbu.T @ xtidx2g
    hb = np.maximum(zb, 0.0)
    haq = mxq(ha, 0, "e4m3")
    hbq = mxq(hb, 0, "e5m2")
    a0 = haq.T @ hbq
    y = 0.04 * (a0 * f64(cw1)).reshape(J, S, I // S).sum(axis=2)
    return y

@@ -1,0 +1,184 @@
+from contextlib import ExitStack
+
+import concourse.mybir as mybir
+
+K, T, J, I, R, S = 512, 512, 256, 256, 512, 64
+FLOPS = 2 * K * R * J + 2 * K * R * I + 2 * R * J * I
+
+F32 = mybir.dt.float32
+BF16 = mybir.dt.bfloat16
+I32 = mybir.dt.int32
+U32 = mybir.dt.uint32
+U16 = mybir.dt.uint16
+U8 = mybir.dt.uint8
+E4M3X4 = mybir.dt.float8_e4m3fn_x4
+E5M2X4 = mybir.dt.float8_e5m2_x4
+E2M1X4 = mybir.dt.float4_e2m1fn_x4
+ALU = mybir.AluOpType
+AXIS_X = mybir.AxisListType.X
+RELU = mybir.ActivationFunctionType.Relu
+
+P = 128
+PACK = 4
+HALF = 128
+BUNDLE = 8
+SET = 4
+BLOCKS = R // 32
+OUT_SCALE = 0.04
+
+
+def tile_list_meet_levelled_plain_summed_kernel(
+    tc, xt_words, xt_scales, wa_words, wa_scales, wb_words, wb_scales, cw1, offs, offs2, out
+):
+    nc = tc.nc
+    with ExitStack() as ctx:
+        sb = ctx.enter_context(tc.tile_pool(name="sb", bufs=1))
+        ps = ctx.enter_context(tc.psum_pool(name="ps", bufs=1))
+
+        def tile(shape, dtype, name):
+            return sb.tile(shape, dtype, name=name, align_bytes=64)
+
+        rows_list = sb.tile([P, J // 16], U16, name="rows_list")
+        cols_list = sb.tile([P, I // 16], U16, name="cols_list")
+        x_words = tile([P, T], U32, "x_words")
+        x_plane = tile([P, T], U8, "x_plane")
+        wa_raw = tile([P, R], U32, "wa_raw")
+        wb_raw = tile([P, R // 2], U32, "wb_raw")
+        wa_plane_raw = tile([P, R], U8, "wa_plane_raw")
+        wb_plane_raw = tile([P, R], U8, "wb_plane_raw")
+        cw_all = tile([P, I], F32, "cw_all")
+
+        def load_plane(engine, plane, scales):
+            for quad in range(4):
+                engine.dma_start(
+                    out=plane[32 * quad : 32 * quad + 4, :].bitcast(I32),
+                    in_=scales[0, 4 * quad : 4 * quad + 4, :].bitcast(I32),
+                )
+
+        for plane in (x_plane, wa_plane_raw, wb_plane_raw):
+            nc.vector.memset(plane[:].bitcast(I32), 0)
+
+        nc.sync.dma_start(out=rows_list[:], in_=offs)
+        nc.sync.dma_start(out=x_words[:].bitcast(I32), in_=xt_words[0].rearrange("p n t -> p (n t)").bitcast(I32))
+        load_plane(nc.sync, x_plane, xt_scales)
+        nc.gpsimd.dma_start(out=wa_raw[:].bitcast(I32), in_=wa_words[0].rearrange("p n t -> p (n t)").bitcast(I32))
+        nc.gpsimd.dma_start(out=wb_raw[:].bitcast(I32), in_=wb_words[0].bitcast(I32))
+        nc.sync.dma_start(out=cols_list[:], in_=offs2)
+        load_plane(nc.sync, wa_plane_raw, wa_scales)
+        load_plane(nc.sync, wb_plane_raw, wb_scales)
+        nc.gpsimd.dma_start(out=cw_all[:], in_=cw1[0].partition_broadcast(P))
+
+        def dealt(raw_words, name):
+            width = raw_words.shape[1]
+            ordered = tile([P, width], U32, name)
+            nc.scalar.copy(
+                out=ordered[:].rearrange("p (t b q) -> p t b q", t=PACK, b=BLOCKS),
+                in_=raw_words.rearrange("p (b t q) -> p t b q", t=PACK, b=BLOCKS),
+            )
+            return ordered
+
+        def gathered(offsets, name):
+            count = offsets.shape[1] * 16
+            words = tile([P, count], U32, name + "_words")
+            plane = tile([P, count], U8, name + "_plane")
+            nc.vector.tensor_copy(out=words[:], in_=x_words[:].indirect(offsets))
+            nc.vector.tensor_copy(out=plane[:], in_=x_plane[:].indirect(offsets))
+            return words, plane
+
+        wa_codes = dealt(wa_raw[:], "wa_codes")
+        wa_plane = dealt(wa_plane_raw[:].bitcast(U32), "wa_plane")
+        xa = [gathered(rows_list[:, 8 * h : 8 * h + 8], "xa%d" % h) for h in range(2)]
+        za = [ps.tile([P, PACK, HALF], F32, name="za%d" % h) for h in range(2)]
+        for h in range(2):
+            for t in range(PACK):
+                nc.tensor.matmul_mx(
+                    out=za[h][:, t, :],
+                    lhsT=wa_codes[:, P * t : P * (t + 1)].bitcast(E5M2X4),
+                    lhsT_scale=wa_plane[:].bitcast(U8)[:, P * t : P * (t + 1)],
+                    rhs=xa[h][0][:].bitcast(E4M3X4),
+                    rhs_scale=xa[h][1][:],
+                    start=True,
+                    stop=True,
+                )
+
+        wb_codes = dealt(wb_raw[:], "wb_codes")
+        wb_plane = dealt(wb_plane_raw[:].bitcast(U32), "wb_plane")
+        xb_words, xb_plane = gathered(cols_list[:], "xb")
+        hb = tile([P, I, PACK], BF16, "hb")
+        for h in range(2):
+            zb = ps.tile([P, PACK, HALF], F32, name="zb%d" % h)
+            cols = slice(HALF * h, HALF * (h + 1))
+            for t in range(PACK):
+                nc.tensor.matmul_mx(
+                    out=zb[:, t, :],
+                    lhsT=wb_codes[:].bitcast(U8)[:, 2 * P * t : 2 * P * (t + 1)].bitcast(E2M1X4),
+                    lhsT_scale=wb_plane[:].bitcast(U8)[:, P * t : P * (t + 1)],
+                    rhs=xb_words[:, cols].bitcast(E4M3X4),
+                    rhs_scale=xb_plane[:, cols],
+                    start=True,
+                    stop=True,
+                )
+            nc.scalar.activation(out=hb[:, cols, :], in_=zb[:].rearrange("p t i -> p i t"), func=RELU)
+
+        bundles = HALF // BUNDLE
+        means = []
+        for h in range(2):
+            sums = tile([P, bundles, PACK], F32, "sums%d" % h)
+            nc.vector.tensor_reduce(
+                out=sums[:], in_=za[h][:].rearrange("p t (e w) -> p e t w", w=BUNDLE), axis=AXIS_X, op=ALU.add
+            )
+            mean = tile([P, bundles, PACK], F32, "mean%d" % h)
+            nc.gpsimd.tensor_scalar(
+                out=mean[:], in0=sums[:], scalar1=1.0 / BUNDLE, scalar2=0.0, op0=ALU.mult, op1=ALU.add
+            )
+            means.append(mean)
+
+        ha = []
+        for h in range(2):
+            centred = tile([P, bundles, BUNDLE, PACK], BF16, "ha%d" % h)
+            nc.vector.tensor_tensor(
+                out=centred[:],
+                in0=za[h][:].rearrange("p t (e w) -> p e w t", w=BUNDLE),
+                in1=means[h][:].unsqueeze(2).to_broadcast([P, bundles, BUNDLE, PACK]),
+                op=ALU.subtract,
+            )
+            ha.append(centred)
+
+        hb_codes = tile([P, I], U32, "hb_codes")
+        hb_plane = tile([P, I], U8, "hb_plane")
+        nc.vector.quantize_mx(
+            out=hb_codes[:].bitcast(E5M2X4), scales=hb_plane[:], in_=hb[:].rearrange("p i t -> p (i t)")
+        )
+        scores = []
+        for h in range(2):
+            ha_codes = tile([P, HALF], U32, "ha_codes%d" % h)
+            ha_plane = tile([P, HALF], U8, "ha_plane%d" % h)
+            nc.vector.quantize_mx(
+                out=ha_codes[:].bitcast(E4M3X4), scales=ha_plane[:], in_=ha[h][:].rearrange("p e w t -> p (e w t)")
+            )
+            a0 = ps.tile([P, I], F32, name="a0_%d" % h)
+            nc.tensor.matmul_mx(
+                out=a0[:],
+                lhsT=ha_codes[:].bitcast(E4M3X4),
+                lhsT_scale=ha_plane[:],
+                rhs=hb_codes[:].bitcast(E5M2X4),
+                rhs_scale=hb_plane[:],
+                start=True,
+                stop=True,
+            )
+            scores.append(a0)
+
+        weighted = []
+        for h in range(2):
+            product = tile([P, I], F32, "weighted%d" % h)
+            nc.vector.scalar_tensor_tensor(
+                out=product[:], in0=scores[h][:], scalar=OUT_SCALE, in1=cw_all[:], op0=ALU.mult, op1=ALU.mult
+            )
+            weighted.append(product)
+        for h in range(2):
+            result = tile([P, S], F32, "result%d" % h)
+            nc.vector.tensor_reduce(
+                out=result[:], in_=weighted[h][:].rearrange("p (s u) -> p s u", u=SET), axis=AXIS_X, op=ALU.add
+            )
+            queue = nc.sync if h == 0 else nc.scalar
+            queue.dma_start(out=out[HALF * h : HALF * (h + 1), :], in_=result[:])

@@ -1,6 +1,7 @@
 from contextlib import ExitStack
 
 import concourse.mybir as mybir
+from concourse.masks import make_identity
 
 K, T, J, I, R, S = 512, 512, 256, 256, 512, 64
 FLOPS = 2 * K * R * J + 2 * K * R * I + 2 * R * J * I
@@ -17,6 +18,7 @@ E2M1X4 = mybir.dt.float4_e2m1fn_x4
 ALU = mybir.AluOpType
 AXIS_X = mybir.AxisListType.X
 RELU = mybir.ActivationFunctionType.Relu
+COPY = mybir.ActivationFunctionType.Copy
 
 P = 128
 PACK = 4
@@ -35,8 +37,8 @@ def tile_list_meet_levelled_plain_summed_kernel(
         sb = ctx.enter_context(tc.tile_pool(name="sb", bufs=1))
         ps = ctx.enter_context(tc.psum_pool(name="ps", bufs=1))
 
-        def tile(shape, dtype, name):
-            return sb.tile(shape, dtype, name=name, align_bytes=64)
+        def tile(shape, dtype, name, tag=None):
+            return sb.tile(shape, dtype, name=name, tag=tag or name, align_bytes=64)
 
         rows_list = sb.tile([P, J // 16], U16, name="rows_list")
         cols_list = sb.tile([P, I // 16], U16, name="cols_list")
@@ -46,7 +48,8 @@ def tile_list_meet_levelled_plain_summed_kernel(
         wb_raw = tile([P, R // 2], U32, "wb_raw")
         wa_plane_raw = tile([P, R], U8, "wa_plane_raw")
         wb_plane_raw = tile([P, R], U8, "wb_plane_raw")
-        cw_all = tile([P, I], F32, "cw_all")
+        cw_pairs = tile([P, 2], F32, "cw_pairs")
+        identity = tile([P, P], F32, "identity")
 
         def load_plane(engine, plane, scales):
             for quad in range(4):
@@ -59,18 +62,20 @@ def tile_list_meet_levelled_plain_summed_kernel(
             nc.vector.memset(plane[:].bitcast(I32), 0)
 
         nc.sync.dma_start(out=rows_list[:], in_=offs)
-        nc.sync.dma_start(out=x_words[:].bitcast(I32), in_=xt_words[0].rearrange("p n t -> p (n t)").bitcast(I32))
+        nc.scalar.dma_start(out=x_words[:].bitcast(I32), in_=xt_words[0].rearrange("p n t -> p (n t)").bitcast(I32))
         load_plane(nc.sync, x_plane, xt_scales)
         nc.gpsimd.dma_start(out=wa_raw[:].bitcast(I32), in_=wa_words[0].rearrange("p n t -> p (n t)").bitcast(I32))
+        nc.vector.memset(identity[:], 0.0)
+        make_identity(nc, identity[:], nomemset=True)
         nc.gpsimd.dma_start(out=wb_raw[:].bitcast(I32), in_=wb_words[0].bitcast(I32))
         nc.sync.dma_start(out=cols_list[:], in_=offs2)
         load_plane(nc.sync, wa_plane_raw, wa_scales)
         load_plane(nc.sync, wb_plane_raw, wb_scales)
-        nc.gpsimd.dma_start(out=cw_all[:], in_=cw1[0].partition_broadcast(P))
+        nc.gpsimd.dma_start(out=cw_pairs[:], in_=cw1[0].rearrange("(p c) -> p c", c=2))
 
-        def dealt(raw_words, name):
+        def dealt(raw_words, name, tag=None):
             width = raw_words.shape[1]
-            ordered = tile([P, width], U32, name)
+            ordered = tile([P, width], U32, name, tag)
             nc.scalar.copy(
                 out=ordered[:].rearrange("p (t b q) -> p t b q", t=PACK, b=BLOCKS),
                 in_=raw_words.rearrange("p (b t q) -> p t b q", t=PACK, b=BLOCKS),
@@ -101,12 +106,12 @@ def tile_list_meet_levelled_plain_summed_kernel(
                     stop=True,
                 )
 
-        wb_codes = dealt(wb_raw[:], "wb_codes")
+        wb_codes = dealt(wb_raw[:], "wb_codes", tag="wa_plane_raw")
         wb_plane = dealt(wb_plane_raw[:].bitcast(U32), "wb_plane")
         xb_words, xb_plane = gathered(cols_list[:], "xb")
         hb = tile([P, I, PACK], BF16, "hb")
         for h in range(2):
-            zb = ps.tile([P, PACK, HALF], F32, name="zb%d" % h)
+            zb = ps.tile([P, PACK, HALF], F32, name="zb%d" % h, tag="zb%d" % h)
             cols = slice(HALF * h, HALF * (h + 1))
             for t in range(PACK):
                 nc.tensor.matmul_mx(
@@ -119,6 +124,12 @@ def tile_list_meet_levelled_plain_summed_kernel(
                     stop=True,
                 )
             nc.scalar.activation(out=hb[:, cols, :], in_=zb[:].rearrange("p t i -> p i t"), func=RELU)
+
+        cw_spread = ps.tile([P, 2, P], F32, name="cw_spread", tag="zb1")
+        for c in range(2):
+            nc.tensor.transpose(cw_spread[:, c, :], cw_pairs[:, c : c + 1].to_broadcast([P, P]), identity[:])
+        cw_all = tile([P, P, 2], F32, "cw_all")
+        nc.scalar.activation(out=cw_all[:], in_=cw_spread[:].rearrange("p c n -> p n c"), func=COPY, scale=OUT_SCALE)
 
         bundles = HALF // BUNDLE
         means = []
@@ -171,8 +182,8 @@ def tile_list_meet_levelled_plain_summed_kernel(
         weighted = []
         for h in range(2):
             product = tile([P, I], F32, "weighted%d" % h)
-            nc.vector.scalar_tensor_tensor(
-                out=product[:], in0=scores[h][:], scalar=OUT_SCALE, in1=cw_all[:], op0=ALU.mult, op1=ALU.mult
+            nc.vector.tensor_tensor(
+                out=product[:], in0=scores[h][:], in1=cw_all[:].rearrange("p n c -> p (n c)"), op=ALU.mult
             )
             weighted.append(product)
         for h in range(2):
@@ -180,5 +191,5 @@ def tile_list_meet_levelled_plain_summed_kernel(
             nc.vector.tensor_reduce(
                 out=result[:], in_=weighted[h][:].rearrange("p (s u) -> p s u", u=SET), axis=AXIS_X, op=ALU.add
             )
-            queue = nc.sync if h == 0 else nc.scalar
+            queue = nc.scalar if h == 0 else nc.sync
             queue.dma_start(out=out[HALF * h : HALF * (h + 1), :], in_=result[:])

from contextlib import ExitStack

import concourse.mybir as mybir
from concourse.masks import make_identity

K, T, J, I, R, S = 512, 512, 256, 256, 512, 64
FLOPS = 2 * K * R * J + 2 * K * R * I + 2 * R * J * I

F32 = mybir.dt.float32
BF16 = mybir.dt.bfloat16
I32 = mybir.dt.int32
U32 = mybir.dt.uint32
U16 = mybir.dt.uint16
U8 = mybir.dt.uint8
E4M3X4 = mybir.dt.float8_e4m3fn_x4
E5M2X4 = mybir.dt.float8_e5m2_x4
E2M1X4 = mybir.dt.float4_e2m1fn_x4
ALU = mybir.AluOpType
AXIS_X = mybir.AxisListType.X
RELU = mybir.ActivationFunctionType.Relu
COPY = mybir.ActivationFunctionType.Copy

P = 128
PACK = 4
HALF = 128
BUNDLE = 8
SET = 4
BLOCKS = R // 32
OUT_SCALE = 0.04


def tile_list_meet_levelled_plain_summed_kernel(
    tc, xt_words, xt_scales, wa_words, wa_scales, wb_words, wb_scales, cw1, offs, offs2, out
):
    nc = tc.nc
    with ExitStack() as ctx:
        sb = ctx.enter_context(tc.tile_pool(name="sb", bufs=1))
        ps = ctx.enter_context(tc.psum_pool(name="ps", bufs=1))

        def tile(shape, dtype, name, tag=None):
            return sb.tile(shape, dtype, name=name, tag=tag or name, align_bytes=64)

        rows_list = sb.tile([P, J // 16], U16, name="rows_list")
        cols_list = sb.tile([P, I // 16], U16, name="cols_list")
        x_words = tile([P, T], U32, "x_words")
        x_plane = tile([P, T], U8, "x_plane")
        wa_raw = tile([P, R], U32, "wa_raw")
        wb_raw = tile([P, R // 2], U32, "wb_raw")
        wa_plane_raw = tile([P, R], U8, "wa_plane_raw")
        wb_plane_raw = tile([P, R], U8, "wb_plane_raw")
        cw_pairs = tile([P, 2], F32, "cw_pairs")
        identity = tile([P, P], F32, "identity")

        def load_plane(engine, plane, scales):
            for quad in range(4):
                engine.dma_start(
                    out=plane[32 * quad : 32 * quad + 4, :].bitcast(I32),
                    in_=scales[0, 4 * quad : 4 * quad + 4, :].bitcast(I32),
                )

        for plane in (x_plane, wa_plane_raw, wb_plane_raw):
            nc.vector.memset(plane[:].bitcast(I32), 0)

        nc.sync.dma_start(out=rows_list[:], in_=offs)
        nc.scalar.dma_start(out=x_words[:].bitcast(I32), in_=xt_words[0].rearrange("p n t -> p (n t)").bitcast(I32))
        load_plane(nc.sync, x_plane, xt_scales)
        nc.gpsimd.dma_start(out=wa_raw[:].bitcast(I32), in_=wa_words[0].rearrange("p n t -> p (n t)").bitcast(I32))
        nc.vector.memset(identity[:], 0.0)
        make_identity(nc, identity[:], nomemset=True)
        nc.gpsimd.dma_start(out=wb_raw[:].bitcast(I32), in_=wb_words[0].bitcast(I32))
        nc.sync.dma_start(out=cols_list[:], in_=offs2)
        load_plane(nc.sync, wa_plane_raw, wa_scales)
        load_plane(nc.sync, wb_plane_raw, wb_scales)
        nc.gpsimd.dma_start(out=cw_pairs[:], in_=cw1[0].rearrange("(p c) -> p c", c=2))

        def dealt(raw_words, name, tag=None):
            width = raw_words.shape[1]
            ordered = tile([P, width], U32, name, tag)
            nc.scalar.copy(
                out=ordered[:].rearrange("p (t b q) -> p t b q", t=PACK, b=BLOCKS),
                in_=raw_words.rearrange("p (b t q) -> p t b q", t=PACK, b=BLOCKS),
            )
            return ordered

        def gathered(offsets, name):
            count = offsets.shape[1] * 16
            words = tile([P, count], U32, name + "_words")
            plane = tile([P, count], U8, name + "_plane")
            nc.vector.tensor_copy(out=words[:], in_=x_words[:].indirect(offsets))
            nc.vector.tensor_copy(out=plane[:], in_=x_plane[:].indirect(offsets))
            return words, plane

        wa_codes = dealt(wa_raw[:], "wa_codes")
        wa_plane = dealt(wa_plane_raw[:].bitcast(U32), "wa_plane")
        xa = [gathered(rows_list[:, 8 * h : 8 * h + 8], "xa%d" % h) for h in range(2)]
        za = [ps.tile([P, PACK, HALF], F32, name="za%d" % h) for h in range(2)]
        for h in range(2):
            for t in range(PACK):
                nc.tensor.matmul_mx(
                    out=za[h][:, t, :],
                    lhsT=wa_codes[:, P * t : P * (t + 1)].bitcast(E5M2X4),
                    lhsT_scale=wa_plane[:].bitcast(U8)[:, P * t : P * (t + 1)],
                    rhs=xa[h][0][:].bitcast(E4M3X4),
                    rhs_scale=xa[h][1][:],
                    start=True,
                    stop=True,
                )

        wb_codes = dealt(wb_raw[:], "wb_codes", tag="wa_plane_raw")
        wb_plane = dealt(wb_plane_raw[:].bitcast(U32), "wb_plane")
        xb_words, xb_plane = gathered(cols_list[:], "xb")
        hb = tile([P, I, PACK], BF16, "hb")
        for h in range(2):
            zb = ps.tile([P, PACK, HALF], F32, name="zb%d" % h, tag="zb%d" % h)
            cols = slice(HALF * h, HALF * (h + 1))
            for t in range(PACK):
                nc.tensor.matmul_mx(
                    out=zb[:, t, :],
                    lhsT=wb_codes[:].bitcast(U8)[:, 2 * P * t : 2 * P * (t + 1)].bitcast(E2M1X4),
                    lhsT_scale=wb_plane[:].bitcast(U8)[:, P * t : P * (t + 1)],
                    rhs=xb_words[:, cols].bitcast(E4M3X4),
                    rhs_scale=xb_plane[:, cols],
                    start=True,
                    stop=True,
                )
            nc.scalar.activation(out=hb[:, cols, :], in_=zb[:].rearrange("p t i -> p i t"), func=RELU)

        cw_spread = ps.tile([P, 2, P], F32, name="cw_spread", tag="zb1")
        for c in range(2):
            nc.tensor.transpose(cw_spread[:, c, :], cw_pairs[:, c : c + 1].to_broadcast([P, P]), identity[:])
        cw_all = tile([P, P, 2], F32, "cw_all")
        nc.scalar.activation(out=cw_all[:], in_=cw_spread[:].rearrange("p c n -> p n c"), func=COPY, scale=OUT_SCALE)

        bundles = HALF // BUNDLE
        means = []
        for h in range(2):
            sums = tile([P, bundles, PACK], F32, "sums%d" % h)
            nc.vector.tensor_reduce(
                out=sums[:], in_=za[h][:].rearrange("p t (e w) -> p e t w", w=BUNDLE), axis=AXIS_X, op=ALU.add
            )
            mean = tile([P, bundles, PACK], F32, "mean%d" % h)
            nc.gpsimd.tensor_scalar(
                out=mean[:], in0=sums[:], scalar1=1.0 / BUNDLE, scalar2=0.0, op0=ALU.mult, op1=ALU.add
            )
            means.append(mean)

        ha = []
        for h in range(2):
            centred = tile([P, bundles, BUNDLE, PACK], BF16, "ha%d" % h)
            nc.vector.tensor_tensor(
                out=centred[:],
                in0=za[h][:].rearrange("p t (e w) -> p e w t", w=BUNDLE),
                in1=means[h][:].unsqueeze(2).to_broadcast([P, bundles, BUNDLE, PACK]),
                op=ALU.subtract,
            )
            ha.append(centred)

        hb_codes = tile([P, I], U32, "hb_codes")
        hb_plane = tile([P, I], U8, "hb_plane")
        nc.vector.quantize_mx(
            out=hb_codes[:].bitcast(E5M2X4), scales=hb_plane[:], in_=hb[:].rearrange("p i t -> p (i t)")
        )
        scores = []
        for h in range(2):
            ha_codes = tile([P, HALF], U32, "ha_codes%d" % h)
            ha_plane = tile([P, HALF], U8, "ha_plane%d" % h)
            nc.vector.quantize_mx(
                out=ha_codes[:].bitcast(E4M3X4), scales=ha_plane[:], in_=ha[h][:].rearrange("p e w t -> p (e w t)")
            )
            a0 = ps.tile([P, I], F32, name="a0_%d" % h)
            nc.tensor.matmul_mx(
                out=a0[:],
                lhsT=ha_codes[:].bitcast(E4M3X4),
                lhsT_scale=ha_plane[:],
                rhs=hb_codes[:].bitcast(E5M2X4),
                rhs_scale=hb_plane[:],
                start=True,
                stop=True,
            )
            scores.append(a0)

        weighted = []
        for h in range(2):
            product = tile([P, I], F32, "weighted%d" % h)
            nc.vector.tensor_tensor(
                out=product[:], in0=scores[h][:], in1=cw_all[:].rearrange("p n c -> p (n c)"), op=ALU.mult
            )
            weighted.append(product)
        for h in range(2):
            result = tile([P, S], F32, "result%d" % h)
            nc.vector.tensor_reduce(
                out=result[:], in_=weighted[h][:].rearrange("p (s u) -> p s u", u=SET), axis=AXIS_X, op=ALU.add
            )
            queue = nc.scalar if h == 0 else nc.sync
            queue.dma_start(out=out[HALF * h : HALF * (h + 1), :], in_=result[:])
